import numpy as np
import ml_dtypes


def mxq(x, axis, fmt="e4m3"):
    dtype, down = {"e4m3": (ml_dtypes.float8_e4m3fn, 7), "e5m2": (ml_dtypes.float8_e5m2, 14)}[fmt]
    v = np.moveaxis(np.asarray(x, np.float32).astype(ml_dtypes.bfloat16).astype(np.float64), axis, -1)
    blocks = v.reshape(v.shape[:-1] + (-1, 32))
    amax = np.abs(blocks).max(-1, keepdims=True)
    byte = np.maximum(np.where(amax > 0, np.frexp(amax)[1] - 1 + 127, 0) - down, 1)
    scale = np.exp2(byte - 127.0)
    codes = (blocks / scale).astype(np.float32).astype(dtype).astype(np.float64)
    return np.moveaxis((codes * scale).reshape(v.shape), -1, axis)


WIDE = False


def mx_kscale(k):
    if not WIDE:
        return np.ones(k)
    levels = np.array([10, -10, 5, -5, 0])
    if k % 512:
        return np.exp2(np.random.permutation(np.resize(levels, k // 32))).repeat(32)
    a = np.empty((k // 512, 16))
    for p in range(k // 512):
        a[p, :8] = np.random.permutation(np.resize(levels, 8))
        for g in range(8):
            far = levels[np.abs(levels - a[p, g]) >= 10]
            a[p, g + 8] = far[np.random.randint(len(far))]
    return np.exp2(a.ravel()).repeat(32)


def f64(x):
    return np.asarray(x).astype(np.float64)


def striped(idx):
    return np.tile(idx.reshape(-1, 16).T, (8, 1)).astype(np.uint16)


def unstriped(offs):
    return offs[:16].T.reshape(-1).astype(np.int64)


def striped8(idx):
    return np.concatenate([x.reshape(-1, 16).T for x in idx]).astype(np.uint16)


def runs(offs, k):
    lists = np.stack([offs[16 * r : 16 * r + 16].T.reshape(-1) for r in range(8)]).astype(np.int64)
    return lists[np.arange(k) % 512 // 64]


def pack_weight(w):
    k, n = w.shape
    w = f64(np.asarray(w, np.float32).astype(ml_dtypes.bfloat16)).reshape(k // 32, 32, n)
    amax = np.abs(w).max(1)
    byte = np.clip(np.where(amax > 0, np.frexp(amax)[1] - 1 + 127 - 7, 1), 1, 254)
    scaled = (w * np.exp2(127.0 - byte)[:, None, :]).reshape(k, n).astype(np.float32)
    words = np.ascontiguousarray(scaled.reshape(k // 512, 128, 4, n).transpose(0, 1, 3, 2)).astype(ml_dtypes.float8_e4m3fn).view(np.uint8)
    return words, np.ascontiguousarray(byte.astype(np.uint8).reshape(k // 512, 16, n))


def unpack_weight(words, scales):
    g, p, n, _ = words.shape
    vals = np.ascontiguousarray(words).view(ml_dtypes.float8_e4m3fn).astype(np.float64) * np.repeat(np.exp2(scales.astype(np.float64) - 127.0), 8, axis=1)[..., None]
    return vals.transpose(0, 1, 3, 2).reshape(g * 512, n)


E2M1 = np.array([0.0, 0.5, 1.0, 1.5, 2.0, 3.0, 4.0, 6.0, -0.0, -0.5, -1.0, -1.5, -2.0, -3.0, -4.0, -6.0])


def pack_fp4(w):
    k, n = w.shape
    w = f64(np.asarray(w, np.float32).astype(ml_dtypes.bfloat16)).reshape(k // 32, 32, n)
    amax = np.abs(w).max(1)
    mant, ex = np.frexp(amax / 6.0)
    byte = np.clip(np.where(amax > 0, np.where(mant > 0.5, ex, ex - 1) + 127, 1), 1, 254)
    scaled = (w * np.exp2(127.0 - byte)[:, None, :]).reshape(k, n).astype(np.float32)
    c = np.ascontiguousarray(scaled.reshape(k // 512, 128, 4, n).transpose(0, 1, 3, 2)).astype(ml_dtypes.float4_e2m1fn).view(np.uint8) & 0xF
    words = (c[..., 0::2] | (c[..., 1::2] << 4)).reshape(k // 512, 128, 2 * n)
    return np.ascontiguousarray(words), np.ascontiguousarray(byte.astype(np.uint8).reshape(k // 512, 16, n))


def unpack_fp4(words, scales):
    g, _, n = scales.shape
    words = np.ascontiguousarray(words).reshape(g, 128, n, 2)
    nib = np.empty((g, 128, n, 4), np.uint8)
    nib[..., 0::2] = words & 0xF
    nib[..., 1::2] = words >> 4
    vals = E2M1[nib] * np.repeat(np.exp2(scales.astype(np.float64) - 127.0), 8, axis=1)[..., None]
    return vals.transpose(0, 1, 3, 2).reshape(g * 512, n)


def planes(y):
    n, m = y.shape
    v = y.astype(np.float32).astype(ml_dtypes.bfloat16).astype(np.float64).reshape(n // 32, 32, m)
    top = np.abs(v).max(1)
    byte = np.clip(np.where(top > 0, np.frexp(top)[1] - 1 + 127 - 7, 1), 1, 254)
    codes = (v * np.exp2(127.0 - byte)[:, None, :]).reshape(n, m).astype(np.float32).astype(ml_dtypes.float8_e4m3fn).view(np.uint8)
    words = codes.reshape(n // 512, 128, 4, m).transpose(0, 1, 3, 2)
    return np.ascontiguousarray(words), np.ascontiguousarray(byte.astype(np.uint8).reshape(n // 512, 16, m))


K, T, S, N, H, W = 512, 2048, 512, 512, 512, 256


def setup_inputs():
    n = np.random.standard_normal
    s = mx_kscale(K)[:, None]
    u = mx_kscale(H)
    packed_xT = pack_weight(n((K, T)) * s)
    packed_w1 = pack_fp4(n((K, H)) / np.sqrt(K) / s)
    packed_w2 = pack_fp4(n((H, N)) / np.sqrt(H) / u[:, None])
    perm = np.stack([np.random.permutation(S) for _ in range(8)])
    return {
        "x_words": packed_xT[0],
        "x_scales": packed_xT[1],
        "w1_words": packed_w1[0],
        "w1_scales": packed_w1[1],
        "gn": (np.random.uniform(0.5, 1.5, (H, 1)) * u[:, None]).astype(np.float32),
        "w2_words": packed_w2[0],
        "w2_scales": packed_w2[1],
        "offs": striped(np.random.permutation(T)[:S]),
        "n1": striped8(perm[:, :W]),
        "n2": striped8(perm[:, W:]),
        "n3": striped8(np.stack([np.random.permutation(S) for _ in range(8)])),
        "n4": striped8(np.stack([np.random.permutation(S) for _ in range(8)])),
    }


def reference(x_words, x_scales, w1_words, w1_scales, gn, w2_words, w2_scales, offs, n1, n2, n3, n4):
    xq = unpack_weight(x_words, x_scales)[:, unstriped(offs)]
    y = unpack_fp4(w1_words, w1_scales).T @ xq
    pb = y[np.arange(H)[:, None], runs(n2, H)]
    pa = y[np.arange(H)[:, None], runs(n1, H)]
    rb = pb - (0.5 * pa)
    ra = np.sqrt((pa) ** 2 + (pb) ** 2 + 0.25)
    ds = np.zeros((H, S))
    ds[np.arange(H)[:, None], runs(n1, H)] = ra
    dt = ds.copy()
    dt[np.arange(H)[:, None], runs(n2, H)] = rb
    z = f64(gn) * dt
    h = unpack_fp4(w2_words, w2_scales).T @ mxq(z, 0, "e4m3")
    out_0 = h * (np.tanh(y[np.arange(H)[:, None], runs(n3, H)] - (y[np.arange(H)[:, None], runs(n4, H)])))
    return (out_0,) + planes(out_0)

@@ -1,0 +1,238 @@
+from contextlib import ExitStack
+
+import concourse.mybir as mybir
+
+K, T, S, N, H, W = 512, 2048, 512, 512, 512, 256
+FLOPS = 2 * K * H * S + 2 * H * N * S
+
+F32 = mybir.dt.float32
+BF16 = mybir.dt.bfloat16
+I32 = mybir.dt.int32
+U32 = mybir.dt.uint32
+U16 = mybir.dt.uint16
+U8 = mybir.dt.uint8
+FP8X4 = mybir.dt.float8_e4m3fn_x4
+FP4X4 = mybir.dt.float4_e2m1fn_x4
+ACT = mybir.ActivationFunctionType
+ALU = mybir.AluOpType
+
+P = 128
+PACK = 4
+LIST = 16
+CHUNKS = (256, 128, 128)
+
+
+def load_scale_rows(engine, plane, scales):
+    for q in range(4):
+        engine.dma_start(out=plane[32 * q : 32 * q + 4, :].bitcast(I32), in_=scales[0, 4 * q : 4 * q + 4, :].bitcast(I32))
+
+
+def deal_columns(nc, words, plane, raw_words, raw_plane):
+    nc.vector.tensor_copy(
+        out=words[:].rearrange("p (t m b) -> p t m b", t=PACK, b=2),
+        in_=raw_words[:].rearrange("p (m t b) -> p t m b", t=PACK, b=2),
+    )
+    nc.vector.tensor_copy(
+        out=plane[:].rearrange("p (t m) -> p t m", t=PACK),
+        in_=raw_plane[:].rearrange("p (m t) -> p t m", t=PACK),
+    )
+
+
+def tile_picked_skipjointbpolar_none_po_kernel(
+    tc, x_words, x_scales, w1_words, w1_scales, gn, w2_words, w2_scales, offs, n1, n2, n3, n4, out_0, out_1, out_2
+):
+    nc = tc.nc
+    with ExitStack() as ctx:
+        sb = ctx.enter_context(tc.tile_pool(name="sb", bufs=1))
+        ps = ctx.enter_context(tc.psum_pool(name="ps", bufs=1))
+
+        def held(name, shape, dtype, tag=None):
+            return sb.tile(shape, dtype, name=name, tag=tag or name, align_bytes=64)
+
+        offs_t = held("offs_t", [P, S // LIST], U16)
+        n1_t = held("n1_t", [P, W // LIST], U16)
+        n2_t = held("n2_t", [P, W // LIST], U16)
+        n3_t = held("n3_t", [P, S // LIST], U16)
+        n4_t = held("n4_t", [P, S // LIST], U16)
+
+        xw = held("xw", [P, T], I32)
+        xs = held("xs", [P, T], U8)
+        w1_raw = held("w1_raw", [P, 2 * H], U8)
+        w1s_raw = held("w1s_raw", [P, H], U8)
+        w2_raw = held("w2_raw", [P, 2 * N], U8)
+        w2s_raw = held("w2s_raw", [P, N], U8)
+        gain = held("gain", [P, PACK], F32)
+
+        nc.vector.memset(xs[:].bitcast(I32), 0)
+        nc.vector.memset(w1s_raw[:].bitcast(I32), 0)
+        nc.gpsimd.memset(w2s_raw[:].bitcast(I32), 0)
+        sixteenth = held("sixteenth", [P, 1], F32)
+        quarter = held("quarter", [P, 1], F32)
+        nc.gpsimd.memset(sixteenth[:], 0.0625)
+        nc.scalar.activation(quarter[:], sixteenth[:], ACT.Sqrt)
+
+        nc.sync.dma_start(out=w1_raw[:].bitcast(I32), in_=w1_words[0].bitcast(I32))
+        nc.sync.dma_start(offs_t[:], offs)
+        load_scale_rows(nc.sync, xs, x_scales)
+        nc.sync.dma_start(out=xw[:], in_=x_words[0].rearrange("p c r -> p (c r)").bitcast(I32))
+        load_scale_rows(nc.scalar, w1s_raw, w1_scales)
+        nc.sync.dma_start(n1_t[:], n1)
+        nc.sync.dma_start(n2_t[:], n2)
+        nc.sync.dma_start(out=w2_raw[:].bitcast(I32), in_=w2_words[0].bitcast(I32))
+        load_scale_rows(nc.gpsimd, w2s_raw, w2_scales)
+        nc.sync.dma_start(out=gain[:], in_=gn.rearrange("(p t) o -> p (t o)", t=PACK))
+        nc.sync.dma_start(n3_t[:], n3)
+        nc.sync.dma_start(n4_t[:], n4)
+
+        w1d = held("w1d", [P, 2 * H], U8)
+        w1sd = held("w1sd", [P, H], U8)
+        xq = held("xq", [P, S], U32)
+        xqs = held("xqs", [P, S], U8)
+
+        deal_columns(nc, w1d, w1sd, w1_raw, w1s_raw)
+        nc.vector.tensor_copy(xqs[:], xs[:].indirect(offs_t[:]))
+        half = S // 2
+        for u in range(2):
+            nc.vector.tensor_copy(
+                xq[:, u * half : (u + 1) * half],
+                xw[:].bitcast(U32).indirect(offs_t[:, u * half // LIST : (u + 1) * half // LIST]),
+            )
+        w2_dealt = held("w2_dealt", [P, 3 * N], U8, tag="xw")
+        w2d, w2sd = w2_dealt[:, : 2 * N], w2_dealt[:, 2 * N :]
+        deal_columns(nc, w2d, w2sd, w2_raw, w2s_raw)
+
+        y = [held("y%d" % t, [P, S], F32) for t in range(PACK)]
+
+        def first_product(t, lo, hi, bank):
+            acc = ps.tile([P, hi - lo], F32, name="acc", tag=bank)
+            nc.tensor.matmul_mx(
+                out=acc[:],
+                lhsT=w1d[:, 2 * P * t : 2 * P * (t + 1)].bitcast(FP4X4),
+                lhsT_scale=w1sd[:, P * t : P * (t + 1)],
+                rhs=xq[:, lo:hi].bitcast(FP8X4),
+                rhs_scale=xqs[:, lo:hi],
+                start=True,
+                stop=True,
+            )
+            nc.scalar.copy(y[t][:, lo:hi], acc[:])
+
+        first_product(0, 0, half, "bank0")
+        first_product(0, half, S, "bank4")
+        for t in range(1, PACK):
+            first_product(t, 0, S, "bank%d" % t)
+
+        pair = [held("pair%d" % t, [P, 2 * W], F32) for t in range(PACK)]
+        square = [held("square%d" % t, [P, 2 * W], F32) for t in range(PACK)]
+        radius2 = [held("radius2_%d" % t, [P, W], F32) for t in range(PACK)]
+        ra = [held("ra%d" % t, [P, W], F32) for t in range(PACK)]
+        dt = [held("dt%d" % t, [P, S], F32) for t in range(PACK)]
+        zb = held("zb", [P, S * PACK], BF16)
+
+        def fetch_pair(t):
+            nc.vector.tensor_scalar(pair[t][:, :W], y[t][:].indirect(n1_t[:]), -0.5, 0.0, ALU.mult, ALU.add)
+            nc.vector.tensor_copy(pair[t][:, W:], y[t][:].indirect(n2_t[:]))
+            nc.scalar.activation(square[t][:], pair[t][:], ACT.Square)
+
+        def put_rb(t):
+            nc.vector.tensor_tensor(dt[t][:].indirect(n2_t[:]), pair[t][:, W:], pair[t][:, :W], ALU.add)
+
+        def root(t):
+            nc.vector.scalar_tensor_tensor(radius2[t][:], square[t][:, :W], 4.0, square[t][:, W:], ALU.mult, ALU.add)
+            nc.scalar.activation(ra[t][:], radius2[t][:], ACT.Sqrt, bias=quarter[:])
+
+        def put_ra(t):
+            nc.vector.tensor_copy(dt[t][:].indirect(n1_t[:]), ra[t][:])
+            nc.scalar.activation(
+                zb[:].rearrange("p (j t) -> p t j", t=PACK)[:, t, :], dt[t][:], ACT.Copy, scale=gain[:, t : t + 1]
+            )
+
+        fetch_pair(0)
+        for t in range(PACK):
+            if t + 1 < PACK:
+                fetch_pair(t + 1)
+            put_rb(t)
+            root(t)
+            if t > 0:
+                put_ra(t - 1)
+        put_ra(PACK - 1)
+
+        zq = held("zq", [P, S], U32)
+        zqs = held("zqs", [P, S], U8)
+        work = held("work", [P, 2 * PACK * S], F32, tag="ra%d" % (PACK - 1))
+        starts = [sum(CHUNKS[:c]) for c in range(len(CHUNKS))]
+        at3_at = [0, 1024, 2048]
+        diff_at = [2048, 3072, 3584]
+        out_rows = out_0.rearrange("(p t) j -> p t j", t=PACK)
+        out_words = out_1[0].rearrange("p c r -> p (c r)").bitcast(I32)
+        oqs = held("oqs", [P, S], U8)
+        res = [held("res%d" % c, [P, PACK * cw], F32) for c, cw in enumerate(CHUNKS)]
+        resb = [held("resb%d" % c, [P, PACK * cw], BF16) for c, cw in enumerate(CHUNKS)]
+        oq = [held("oq%d" % c, [P, cw], U32) for c, cw in enumerate(CHUNKS)]
+
+        def fetch_factor(c):
+            lo, cw = starts[c], CHUNKS[c]
+            cols = slice(lo // LIST, (lo + cw) // LIST)
+            for t in range(PACK):
+                a = at3_at[c] + t * cw
+                nc.vector.tensor_copy(work[:, a : a + cw], y[t][:].indirect(n4_t[:, cols]))
+            for t in range(PACK):
+                a, d = at3_at[c] + t * cw, diff_at[c] + t * cw
+                nc.vector.tensor_tensor(work[:, d : d + cw], y[t][:].indirect(n3_t[:, cols]), work[:, a : a + cw], ALU.subtract)
+            for b in range(PACK * cw // 512):
+                d = diff_at[c] + 512 * b
+                nc.scalar.activation(work[:, d : d + 512], work[:, d : d + 512], ACT.Tanh)
+
+        banks = {}
+
+        def second_product(c):
+            lo, cw = starts[c], CHUNKS[c]
+            per_bank = 512 // cw
+            for b in range(PACK // per_bank):
+                name = "bank%d" % ((5 + lo // 128 + b) % 8)
+                acc = ps.tile([P, 512], F32, name="hacc", tag=name)
+                banks[(c, b)] = acc
+                for i in range(per_bank):
+                    t = b * per_bank + i
+                    nc.tensor.matmul_mx(
+                        out=acc[:, i * cw : (i + 1) * cw],
+                        lhsT=w2d[:, 2 * P * t : 2 * P * (t + 1)].bitcast(FP4X4),
+                        lhsT_scale=w2sd[:, P * t : P * (t + 1)],
+                        rhs=zq[:, lo : lo + cw].bitcast(FP8X4),
+                        rhs_scale=zqs[:, lo : lo + cw],
+                        start=True,
+                        stop=True,
+                    )
+
+        def multiply(c, last):
+            lo, cw = starts[c], CHUNKS[c]
+            for b in range(PACK * cw // 512):
+                d = diff_at[c] + 512 * b
+                nc.vector.tensor_tensor(res[c][:, 512 * b : 512 * (b + 1)], banks[(c, b)][:], work[:, d : d + 512], ALU.mult)
+            nc.sync.dma_start(out=out_rows[:, :, lo : lo + cw], in_=res[c][:].rearrange("p (t j) -> p t j", t=PACK))
+            grouped = resb[c][:].rearrange("p (j t) -> p j t", t=PACK)
+            planes = res[c][:].rearrange("p (t j) -> p j t", t=PACK)
+            if last:
+                nc.vector.tensor_copy(grouped, planes)
+            else:
+                nc.scalar.copy(grouped, planes)
+
+        def hand_on(c):
+            lo, cw = starts[c], CHUNKS[c]
+            nc.vector.quantize_mx(out=oq[c][:].bitcast(FP8X4), scales=oqs[:, lo : lo + cw], in_=resb[c][:])
+            nc.sync.dma_start(out=out_words[:, lo : lo + cw], in_=oq[c][:].bitcast(I32))
+
+        fetch_factor(0)
+        nc.vector.quantize_mx(out=zq[:].bitcast(FP8X4), scales=zqs[:], in_=zb[:])
+        for c in range(len(CHUNKS)):
+            second_product(c)
+        fetch_factor(1)
+        multiply(0, False)
+        fetch_factor(2)
+        hand_on(0)
+        multiply(1, False)
+        multiply(2, True)
+        hand_on(1)
+        hand_on(2)
+        for q in range(4):
+            engine = nc.scalar if q % 2 else nc.sync
+            engine.dma_start(out=out_2[0, 4 * q : 4 * q + 4, :].bitcast(I32), in_=oqs[32 * q : 32 * q + 4, :].bitcast(I32))

@@ -1,6 +1,7 @@
 from contextlib import ExitStack
 
 import concourse.mybir as mybir
+from concourse.masks import make_identity
 
 K, T, S, N, H, W = 512, 2048, 512, 512, 512, 256
 FLOPS = 2 * K * H * S + 2 * H * N * S
@@ -20,6 +21,7 @@ P = 128
 PACK = 4
 LIST = 16
 CHUNKS = (256, 128, 128)
+UNIT = 512
 
 
 def load_scale_rows(engine, plane, scales):
@@ -27,11 +29,14 @@ def load_scale_rows(engine, plane, scales):
         engine.dma_start(out=plane[32 * q : 32 * q + 4, :].bitcast(I32), in_=scales[0, 4 * q : 4 * q + 4, :].bitcast(I32))
 
 
-def deal_columns(nc, words, plane, raw_words, raw_plane):
+def deal_words(nc, words, raw_words):
     nc.vector.tensor_copy(
         out=words[:].rearrange("p (t m b) -> p t m b", t=PACK, b=2),
         in_=raw_words[:].rearrange("p (m t b) -> p t m b", t=PACK, b=2),
     )
+
+
+def deal_plane(nc, plane, raw_plane):
     nc.vector.tensor_copy(
         out=plane[:].rearrange("p (t m) -> p t m", t=PACK),
         in_=raw_plane[:].rearrange("p (m t) -> p t m", t=PACK),
@@ -62,34 +67,36 @@ def tile_picked_skipjointbpolar_none_po_kernel(
         w2_raw = held("w2_raw", [P, 2 * N], U8)
         w2s_raw = held("w2s_raw", [P, N], U8)
         gain = held("gain", [P, PACK], F32)
+        sixteenth = held("sixteenth", [P, 1], F32)
+        quarter = held("quarter", [P, 1], F32)
+        ident = held("ident", [P, P], F32)
 
         nc.vector.memset(xs[:].bitcast(I32), 0)
         nc.vector.memset(w1s_raw[:].bitcast(I32), 0)
+        nc.vector.memset(sixteenth[:], 0.0625)
+        make_identity(nc, ident[:])
         nc.gpsimd.memset(w2s_raw[:].bitcast(I32), 0)
-        sixteenth = held("sixteenth", [P, 1], F32)
-        quarter = held("quarter", [P, 1], F32)
-        nc.gpsimd.memset(sixteenth[:], 0.0625)
-        nc.scalar.activation(quarter[:], sixteenth[:], ACT.Sqrt)
 
-        nc.sync.dma_start(out=w1_raw[:].bitcast(I32), in_=w1_words[0].bitcast(I32))
         nc.sync.dma_start(offs_t[:], offs)
+        nc.sync.dma_start(out=w1_raw[:].bitcast(I32), in_=w1_words[0].bitcast(I32))
         load_scale_rows(nc.sync, xs, x_scales)
         nc.sync.dma_start(out=xw[:], in_=x_words[0].rearrange("p c r -> p (c r)").bitcast(I32))
-        load_scale_rows(nc.scalar, w1s_raw, w1_scales)
+        load_scale_rows(nc.sync, w1s_raw, w1_scales)
+        nc.scalar.activation(quarter[:], sixteenth[:], ACT.Sqrt)
         nc.sync.dma_start(n1_t[:], n1)
         nc.sync.dma_start(n2_t[:], n2)
         nc.sync.dma_start(out=w2_raw[:].bitcast(I32), in_=w2_words[0].bitcast(I32))
-        load_scale_rows(nc.gpsimd, w2s_raw, w2_scales)
-        nc.sync.dma_start(out=gain[:], in_=gn.rearrange("(p t) o -> p (t o)", t=PACK))
+        load_scale_rows(nc.sync, w2s_raw, w2_scales)
         nc.sync.dma_start(n3_t[:], n3)
         nc.sync.dma_start(n4_t[:], n4)
+        nc.sync.dma_start(out=gain[:], in_=gn.rearrange("(p t) o -> p (t o)", t=PACK))
 
         w1d = held("w1d", [P, 2 * H], U8)
         w1sd = held("w1sd", [P, H], U8)
         xq = held("xq", [P, S], U32)
         xqs = held("xqs", [P, S], U8)
 
-        deal_columns(nc, w1d, w1sd, w1_raw, w1s_raw)
+        deal_words(nc, w1d, w1_raw)
         nc.vector.tensor_copy(xqs[:], xs[:].indirect(offs_t[:]))
         half = S // 2
         for u in range(2):
@@ -97,9 +104,12 @@ def tile_picked_skipjointbpolar_none_po_kernel(
                 xq[:, u * half : (u + 1) * half],
                 xw[:].bitcast(U32).indirect(offs_t[:, u * half // LIST : (u + 1) * half // LIST]),
             )
+            if u == 0:
+                deal_plane(nc, w1sd, w1s_raw)
         w2_dealt = held("w2_dealt", [P, 3 * N], U8, tag="xw")
         w2d, w2sd = w2_dealt[:, : 2 * N], w2_dealt[:, 2 * N :]
-        deal_columns(nc, w2d, w2sd, w2_raw, w2s_raw)
+        deal_words(nc, w2d, w2_raw)
+        deal_plane(nc, w2sd, w2s_raw)
 
         y = [held("y%d" % t, [P, S], F32) for t in range(PACK)]
 
@@ -126,19 +136,32 @@ def tile_picked_skipjointbpolar_none_po_kernel(
         radius2 = [held("radius2_%d" % t, [P, W], F32) for t in range(PACK)]
         ra = [held("ra%d" % t, [P, W], F32) for t in range(PACK)]
         dt = [held("dt%d" % t, [P, S], F32) for t in range(PACK)]
-        zb = held("zb", [P, S * PACK], BF16)
+
+        def turn_sum(bank, first, second, width):
+            for s in range(0, width, P):
+                nc.tensor.matmul(bank[:, s : s + P], first[:, s : s + P], ident[:], start=True, stop=False, is_transpose=True)
+                nc.tensor.matmul(bank[:, s : s + P], second[:, s : s + P], ident[:], start=False, stop=True, is_transpose=True)
+
+        def turn(bank, src, width):
+            for s in range(0, width, P):
+                nc.tensor.transpose(bank[:, s : s + P], src[:, s : s + P], ident[:])
 
         def fetch_pair(t):
             nc.vector.tensor_scalar(pair[t][:, :W], y[t][:].indirect(n1_t[:]), -0.5, 0.0, ALU.mult, ALU.add)
             nc.vector.tensor_copy(pair[t][:, W:], y[t][:].indirect(n2_t[:]))
-            nc.scalar.activation(square[t][:], pair[t][:], ACT.Square)
+            nc.scalar.activation(square[t][:, :W], pair[t][:, :W], ACT.Square, scale=2.0)
+            nc.scalar.activation(square[t][:, W:], pair[t][:, W:], ACT.Square)
 
         def put_rb(t):
             nc.vector.tensor_tensor(dt[t][:].indirect(n2_t[:]), pair[t][:, W:], pair[t][:, :W], ALU.add)
 
         def root(t):
-            nc.vector.scalar_tensor_tensor(radius2[t][:], square[t][:, :W], 4.0, square[t][:, W:], ALU.mult, ALU.add)
-            nc.scalar.activation(ra[t][:], radius2[t][:], ACT.Sqrt, bias=quarter[:])
+            total = ps.tile([P, W], F32, name="total", tag="bank%d" % (5 + t % 2))
+            turn_sum(total, square[t][:, :W], square[t][:, W:], W)
+            nc.scalar.activation(radius2[t][:], total[:], ACT.Sqrt, bias=quarter[:])
+            back = ps.tile([P, W], F32, name="back", tag="bank%d" % ((7 + t % 2) % 8))
+            turn(back, radius2[t][:], W)
+            nc.scalar.copy(ra[t][:], back[:])
 
         def put_ra(t):
             nc.vector.tensor_copy(dt[t][:].indirect(n1_t[:]), ra[t][:])
@@ -152,62 +175,59 @@ def tile_picked_skipjointbpolar_none_po_kernel(
                 fetch_pair(t + 1)
             put_rb(t)
             root(t)
-            if t > 0:
-                put_ra(t - 1)
-        put_ra(PACK - 1)
+        zb = held("zb", [P, S * PACK], BF16, tag="radius2_%d" % (PACK - 1))
+        for t in range(PACK):
+            put_ra(t)
 
         zq = held("zq", [P, S], U32)
         zqs = held("zqs", [P, S], U8)
-        work = held("work", [P, 2 * PACK * S], F32, tag="ra%d" % (PACK - 1))
-        starts = [sum(CHUNKS[:c]) for c in range(len(CHUNKS))]
-        at3_at = [0, 1024, 2048]
-        diff_at = [2048, 3072, 3584]
         out_rows = out_0.rearrange("(p t) j -> p t j", t=PACK)
         out_words = out_1[0].rearrange("p c r -> p (c r)").bitcast(I32)
         oqs = held("oqs", [P, S], U8)
+        starts = [sum(CHUNKS[:c]) for c in range(len(CHUNKS))]
         res = [held("res%d" % c, [P, PACK * cw], F32) for c, cw in enumerate(CHUNKS)]
         resb = [held("resb%d" % c, [P, PACK * cw], BF16) for c, cw in enumerate(CHUNKS)]
         oq = [held("oq%d" % c, [P, cw], U32) for c, cw in enumerate(CHUNKS)]
+        units = [(0, 0, 2), (0, 2, 2), (1, 0, 4), (2, 0, 4)]
 
-        def fetch_factor(c):
+        def fetch_factor(u, at4, diff):
+            c, t0, nt = units[u]
             lo, cw = starts[c], CHUNKS[c]
             cols = slice(lo // LIST, (lo + cw) // LIST)
-            for t in range(PACK):
-                a = at3_at[c] + t * cw
-                nc.vector.tensor_copy(work[:, a : a + cw], y[t][:].indirect(n4_t[:, cols]))
-            for t in range(PACK):
-                a, d = at3_at[c] + t * cw, diff_at[c] + t * cw
-                nc.vector.tensor_tensor(work[:, d : d + cw], y[t][:].indirect(n3_t[:, cols]), work[:, a : a + cw], ALU.subtract)
-            for b in range(PACK * cw // 512):
-                d = diff_at[c] + 512 * b
-                nc.scalar.activation(work[:, d : d + 512], work[:, d : d + 512], ACT.Tanh)
+            for i in range(nt):
+                nc.vector.tensor_copy(at4[:, i * cw : (i + 1) * cw], y[t0 + i][:].indirect(n4_t[:, cols]))
+            for i in range(nt):
+                nc.vector.tensor_tensor(
+                    diff[:, i * cw : (i + 1) * cw], y[t0 + i][:].indirect(n3_t[:, cols]), at4[:, i * cw : (i + 1) * cw], ALU.subtract
+                )
+            for b in range(2):
+                nc.scalar.activation(diff[:, b * 256 : (b + 1) * 256], diff[:, b * 256 : (b + 1) * 256], ACT.Tanh)
+            return diff
 
-        banks = {}
-
-        def second_product(c):
+        def second_product(u):
+            c, t0, nt = units[u]
             lo, cw = starts[c], CHUNKS[c]
-            per_bank = 512 // cw
-            for b in range(PACK // per_bank):
-                name = "bank%d" % ((5 + lo // 128 + b) % 8)
-                acc = ps.tile([P, 512], F32, name="hacc", tag=name)
-                banks[(c, b)] = acc
-                for i in range(per_bank):
-                    t = b * per_bank + i
-                    nc.tensor.matmul_mx(
-                        out=acc[:, i * cw : (i + 1) * cw],
-                        lhsT=w2d[:, 2 * P * t : 2 * P * (t + 1)].bitcast(FP4X4),
-                        lhsT_scale=w2sd[:, P * t : P * (t + 1)],
-                        rhs=zq[:, lo : lo + cw].bitcast(FP8X4),
-                        rhs_scale=zqs[:, lo : lo + cw],
-                        start=True,
-                        stop=True,
-                    )
+            acc = ps.tile([P, UNIT], F32, name="hacc", tag="bank%d" % (1 + u))
+            for i in range(nt):
+                t = t0 + i
+                nc.tensor.matmul_mx(
+                    out=acc[:, i * cw : (i + 1) * cw],
+                    lhsT=w2d[:, 2 * P * t : 2 * P * (t + 1)].bitcast(FP4X4),
+                    lhsT_scale=w2sd[:, P * t : P * (t + 1)],
+                    rhs=zq[:, lo : lo + cw].bitcast(FP8X4),
+                    rhs_scale=zqs[:, lo : lo + cw],
+                    start=True,
+                    stop=True,
+                )
+            return acc
 
-        def multiply(c, last):
+        def multiply(u, factor):
+            c, t0, nt = units[u]
+            cw = CHUNKS[c]
+            nc.vector.tensor_tensor(res[c][:, t0 * cw : (t0 + nt) * cw], h[u][:], factor, ALU.mult)
+
+        def store(c, last):
             lo, cw = starts[c], CHUNKS[c]
-            for b in range(PACK * cw // 512):
-                d = diff_at[c] + 512 * b
-                nc.vector.tensor_tensor(res[c][:, 512 * b : 512 * (b + 1)], banks[(c, b)][:], work[:, d : d + 512], ALU.mult)
             nc.sync.dma_start(out=out_rows[:, :, lo : lo + cw], in_=res[c][:].rearrange("p (t j) -> p t j", t=PACK))
             grouped = resb[c][:].rearrange("p (j t) -> p j t", t=PACK)
             planes = res[c][:].rearrange("p (t j) -> p j t", t=PACK)
@@ -216,23 +236,29 @@ def tile_picked_skipjointbpolar_none_po_kernel(
             else:
                 nc.scalar.copy(grouped, planes)
 
-        def hand_on(c):
+        def hand_on(c, queue):
             lo, cw = starts[c], CHUNKS[c]
             nc.vector.quantize_mx(out=oq[c][:].bitcast(FP8X4), scales=oqs[:, lo : lo + cw], in_=resb[c][:])
-            nc.sync.dma_start(out=out_words[:, lo : lo + cw], in_=oq[c][:].bitcast(I32))
+            queue.dma_start(out=out_words[:, lo : lo + cw], in_=oq[c][:].bitcast(I32))
 
-        fetch_factor(0)
+        early = held("early", [P, 2 * UNIT], F32, tag="ra%d" % (PACK - 1))
+        f0 = fetch_factor(0, early[:, :UNIT], early[:, UNIT:])
         nc.vector.quantize_mx(out=zq[:].bitcast(FP8X4), scales=zqs[:], in_=zb[:])
-        for c in range(len(CHUNKS)):
-            second_product(c)
-        fetch_factor(1)
-        multiply(0, False)
-        fetch_factor(2)
-        hand_on(0)
-        multiply(1, False)
-        multiply(2, True)
-        hand_on(1)
-        hand_on(2)
+        h = [second_product(u) for u in range(4)]
+        later = held("later", [P, 4 * UNIT], F32, tag="radius2_%d" % (PACK - 1))
+        f1 = fetch_factor(1, later[:, :UNIT], later[:, UNIT : 2 * UNIT])
+        f2 = fetch_factor(2, later[:, 2 * UNIT : 3 * UNIT], later[:, 3 * UNIT :])
+        multiply(0, f0)
+        multiply(1, f1)
+        store(0, False)
+        f3 = fetch_factor(3, f0, f1)
+        multiply(2, f2)
+        store(1, False)
+        hand_on(0, nc.sync)
+        multiply(3, f3)
+        store(2, True)
+        hand_on(1, nc.sync)
+        hand_on(2, nc.scalar)
         for q in range(4):
-            engine = nc.scalar if q % 2 else nc.sync
-            engine.dma_start(out=out_2[0, 4 * q : 4 * q + 4, :].bitcast(I32), in_=oqs[32 * q : 32 * q + 4, :].bitcast(I32))
+            queue = nc.scalar if q % 2 else nc.sync
+            queue.dma_start(out=out_2[0, 4 * q : 4 * q + 4, :].bitcast(I32), in_=oqs[32 * q : 32 * q + 4, :].bitcast(I32))

from contextlib import ExitStack

import concourse.mybir as mybir
from concourse.masks import make_identity

K, T, S, N, H, W = 512, 2048, 512, 512, 512, 256
FLOPS = 2 * K * H * S + 2 * H * N * S

F32 = mybir.dt.float32
BF16 = mybir.dt.bfloat16
I32 = mybir.dt.int32
U32 = mybir.dt.uint32
U16 = mybir.dt.uint16
U8 = mybir.dt.uint8
FP8X4 = mybir.dt.float8_e4m3fn_x4
FP4X4 = mybir.dt.float4_e2m1fn_x4
ACT = mybir.ActivationFunctionType
ALU = mybir.AluOpType

P = 128
PACK = 4
LIST = 16
CHUNKS = (256, 128, 128)
UNIT = 512


def load_scale_rows(engine, plane, scales):
    for q in range(4):
        engine.dma_start(out=plane[32 * q : 32 * q + 4, :].bitcast(I32), in_=scales[0, 4 * q : 4 * q + 4, :].bitcast(I32))


def deal_words(nc, words, raw_words):
    nc.vector.tensor_copy(
        out=words[:].rearrange("p (t m b) -> p t m b", t=PACK, b=2),
        in_=raw_words[:].rearrange("p (m t b) -> p t m b", t=PACK, b=2),
    )


def deal_plane(nc, plane, raw_plane):
    nc.vector.tensor_copy(
        out=plane[:].rearrange("p (t m) -> p t m", t=PACK),
        in_=raw_plane[:].rearrange("p (m t) -> p t m", t=PACK),
    )


def tile_picked_skipjointbpolar_none_po_kernel(
    tc, x_words, x_scales, w1_words, w1_scales, gn, w2_words, w2_scales, offs, n1, n2, n3, n4, out_0, out_1, out_2
):
    nc = tc.nc
    with ExitStack() as ctx:
        sb = ctx.enter_context(tc.tile_pool(name="sb", bufs=1))
        ps = ctx.enter_context(tc.psum_pool(name="ps", bufs=1))

        def held(name, shape, dtype, tag=None):
            return sb.tile(shape, dtype, name=name, tag=tag or name, align_bytes=64)

        offs_t = held("offs_t", [P, S // LIST], U16)
        n1_t = held("n1_t", [P, W // LIST], U16)
        n2_t = held("n2_t", [P, W // LIST], U16)
        n3_t = held("n3_t", [P, S // LIST], U16)
        n4_t = held("n4_t", [P, S // LIST], U16)

        xw = held("xw", [P, T], I32)
        xs = held("xs", [P, T], U8)
        w1_raw = held("w1_raw", [P, 2 * H], U8)
        w1s_raw = held("w1s_raw", [P, H], U8)
        w2_raw = held("w2_raw", [P, 2 * N], U8)
        w2s_raw = held("w2s_raw", [P, N], U8)
        gain = held("gain", [P, PACK], F32)
        sixteenth = held("sixteenth", [P, 1], F32)
        quarter = held("quarter", [P, 1], F32)
        ident = held("ident", [P, P], F32)

        nc.vector.memset(xs[:].bitcast(I32), 0)
        nc.vector.memset(w1s_raw[:].bitcast(I32), 0)
        nc.vector.memset(sixteenth[:], 0.0625)
        make_identity(nc, ident[:])
        nc.gpsimd.memset(w2s_raw[:].bitcast(I32), 0)

        nc.sync.dma_start(offs_t[:], offs)
        nc.sync.dma_start(out=w1_raw[:].bitcast(I32), in_=w1_words[0].bitcast(I32))
        load_scale_rows(nc.sync, xs, x_scales)
        nc.sync.dma_start(out=xw[:], in_=x_words[0].rearrange("p c r -> p (c r)").bitcast(I32))
        load_scale_rows(nc.sync, w1s_raw, w1_scales)
        nc.scalar.activation(quarter[:], sixteenth[:], ACT.Sqrt)
        nc.sync.dma_start(n1_t[:], n1)
        nc.sync.dma_start(n2_t[:], n2)
        nc.sync.dma_start(out=w2_raw[:].bitcast(I32), in_=w2_words[0].bitcast(I32))
        load_scale_rows(nc.sync, w2s_raw, w2_scales)
        nc.sync.dma_start(n3_t[:], n3)
        nc.sync.dma_start(n4_t[:], n4)
        nc.sync.dma_start(out=gain[:], in_=gn.rearrange("(p t) o -> p (t o)", t=PACK))

        w1d = held("w1d", [P, 2 * H], U8)
        w1sd = held("w1sd", [P, H], U8)
        xq = held("xq", [P, S], U32)
        xqs = held("xqs", [P, S], U8)

        deal_words(nc, w1d, w1_raw)
        nc.vector.tensor_copy(xqs[:], xs[:].indirect(offs_t[:]))
        half = S // 2
        for u in range(2):
            nc.vector.tensor_copy(
                xq[:, u * half : (u + 1) * half],
                xw[:].bitcast(U32).indirect(offs_t[:, u * half // LIST : (u + 1) * half // LIST]),
            )
            if u == 0:
                deal_plane(nc, w1sd, w1s_raw)
        w2_dealt = held("w2_dealt", [P, 3 * N], U8, tag="xw")
        w2d, w2sd = w2_dealt[:, : 2 * N], w2_dealt[:, 2 * N :]
        deal_words(nc, w2d, w2_raw)
        deal_plane(nc, w2sd, w2s_raw)

        y = [held("y%d" % t, [P, S], F32) for t in range(PACK)]

        def first_product(t, lo, hi, bank):
            acc = ps.tile([P, hi - lo], F32, name="acc", tag=bank)
            nc.tensor.matmul_mx(
                out=acc[:],
                lhsT=w1d[:, 2 * P * t : 2 * P * (t + 1)].bitcast(FP4X4),
                lhsT_scale=w1sd[:, P * t : P * (t + 1)],
                rhs=xq[:, lo:hi].bitcast(FP8X4),
                rhs_scale=xqs[:, lo:hi],
                start=True,
                stop=True,
            )
            nc.scalar.copy(y[t][:, lo:hi], acc[:])

        first_product(0, 0, half, "bank0")
        first_product(0, half, S, "bank4")
        for t in range(1, PACK):
            first_product(t, 0, S, "bank%d" % t)

        pair = [held("pair%d" % t, [P, 2 * W], F32) for t in range(PACK)]
        square = [held("square%d" % t, [P, 2 * W], F32) for t in range(PACK)]
        radius2 = [held("radius2_%d" % t, [P, W], F32) for t in range(PACK)]
        ra = [held("ra%d" % t, [P, W], F32) for t in range(PACK)]
        dt = [held("dt%d" % t, [P, S], F32) for t in range(PACK)]

        def turn_sum(bank, first, second, width):
            for s in range(0, width, P):
                nc.tensor.matmul(bank[:, s : s + P], first[:, s : s + P], ident[:], start=True, stop=False, is_transpose=True)
                nc.tensor.matmul(bank[:, s : s + P], second[:, s : s + P], ident[:], start=False, stop=True, is_transpose=True)

        def turn(bank, src, width):
            for s in range(0, width, P):
                nc.tensor.transpose(bank[:, s : s + P], src[:, s : s + P], ident[:])

        def fetch_pair(t):
            nc.vector.tensor_scalar(pair[t][:, :W], y[t][:].indirect(n1_t[:]), -0.5, 0.0, ALU.mult, ALU.add)
            nc.vector.tensor_copy(pair[t][:, W:], y[t][:].indirect(n2_t[:]))
            nc.scalar.activation(square[t][:, :W], pair[t][:, :W], ACT.Square, scale=2.0)
            nc.scalar.activation(square[t][:, W:], pair[t][:, W:], ACT.Square)

        def put_rb(t):
            nc.vector.tensor_tensor(dt[t][:].indirect(n2_t[:]), pair[t][:, W:], pair[t][:, :W], ALU.add)

        def root(t):
            total = ps.tile([P, W], F32, name="total", tag="bank%d" % (5 + t % 2))
            turn_sum(total, square[t][:, :W], square[t][:, W:], W)
            nc.scalar.activation(radius2[t][:], total[:], ACT.Sqrt, bias=quarter[:])
            back = ps.tile([P, W], F32, name="back", tag="bank%d" % ((7 + t % 2) % 8))
            turn(back, radius2[t][:], W)
            nc.scalar.copy(ra[t][:], back[:])

        def put_ra(t):
            nc.vector.tensor_copy(dt[t][:].indirect(n1_t[:]), ra[t][:])
            nc.scalar.activation(
                zb[:].rearrange("p (j t) -> p t j", t=PACK)[:, t, :], dt[t][:], ACT.Copy, scale=gain[:, t : t + 1]
            )

        fetch_pair(0)
        for t in range(PACK):
            if t + 1 < PACK:
                fetch_pair(t + 1)
            put_rb(t)
            root(t)
        zb = held("zb", [P, S * PACK], BF16, tag="radius2_%d" % (PACK - 1))
        for t in range(PACK):
            put_ra(t)

        zq = held("zq", [P, S], U32)
        zqs = held("zqs", [P, S], U8)
        out_rows = out_0.rearrange("(p t) j -> p t j", t=PACK)
        out_words = out_1[0].rearrange("p c r -> p (c r)").bitcast(I32)
        oqs = held("oqs", [P, S], U8)
        starts = [sum(CHUNKS[:c]) for c in range(len(CHUNKS))]
        res = [held("res%d" % c, [P, PACK * cw], F32) for c, cw in enumerate(CHUNKS)]
        resb = [held("resb%d" % c, [P, PACK * cw], BF16) for c, cw in enumerate(CHUNKS)]
        oq = [held("oq%d" % c, [P, cw], U32) for c, cw in enumerate(CHUNKS)]
        units = [(0, 0, 2), (0, 2, 2), (1, 0, 4), (2, 0, 4)]

        def fetch_factor(u, at4, diff):
            c, t0, nt = units[u]
            lo, cw = starts[c], CHUNKS[c]
            cols = slice(lo // LIST, (lo + cw) // LIST)
            for i in range(nt):
                nc.vector.tensor_copy(at4[:, i * cw : (i + 1) * cw], y[t0 + i][:].indirect(n4_t[:, cols]))
            for i in range(nt):
                nc.vector.tensor_tensor(
                    diff[:, i * cw : (i + 1) * cw], y[t0 + i][:].indirect(n3_t[:, cols]), at4[:, i * cw : (i + 1) * cw], ALU.subtract
                )
            for b in range(2):
                nc.scalar.activation(diff[:, b * 256 : (b + 1) * 256], diff[:, b * 256 : (b + 1) * 256], ACT.Tanh)
            return diff

        def second_product(u):
            c, t0, nt = units[u]
            lo, cw = starts[c], CHUNKS[c]
            acc = ps.tile([P, UNIT], F32, name="hacc", tag="bank%d" % (1 + u))
            for i in range(nt):
                t = t0 + i
                nc.tensor.matmul_mx(
                    out=acc[:, i * cw : (i + 1) * cw],
                    lhsT=w2d[:, 2 * P * t : 2 * P * (t + 1)].bitcast(FP4X4),
                    lhsT_scale=w2sd[:, P * t : P * (t + 1)],
                    rhs=zq[:, lo : lo + cw].bitcast(FP8X4),
                    rhs_scale=zqs[:, lo : lo + cw],
                    start=True,
                    stop=True,
                )
            return acc

        def multiply(u, factor):
            c, t0, nt = units[u]
            cw = CHUNKS[c]
            nc.vector.tensor_tensor(res[c][:, t0 * cw : (t0 + nt) * cw], h[u][:], factor, ALU.mult)

        def store(c, last):
            lo, cw = starts[c], CHUNKS[c]
            nc.sync.dma_start(out=out_rows[:, :, lo : lo + cw], in_=res[c][:].rearrange("p (t j) -> p t j", t=PACK))
            grouped = resb[c][:].rearrange("p (j t) -> p j t", t=PACK)
            planes = res[c][:].rearrange("p (t j) -> p j t", t=PACK)
            if last:
                nc.vector.tensor_copy(grouped, planes)
            else:
                nc.scalar.copy(grouped, planes)

        def hand_on(c, queue):
            lo, cw = starts[c], CHUNKS[c]
            nc.vector.quantize_mx(out=oq[c][:].bitcast(FP8X4), scales=oqs[:, lo : lo + cw], in_=resb[c][:])
            queue.dma_start(out=out_words[:, lo : lo + cw], in_=oq[c][:].bitcast(I32))

        early = held("early", [P, 2 * UNIT], F32, tag="ra%d" % (PACK - 1))
        f0 = fetch_factor(0, early[:, :UNIT], early[:, UNIT:])
        nc.vector.quantize_mx(out=zq[:].bitcast(FP8X4), scales=zqs[:], in_=zb[:])
        h = [second_product(u) for u in range(4)]
        later = held("later", [P, 4 * UNIT], F32, tag="radius2_%d" % (PACK - 1))
        f1 = fetch_factor(1, later[:, :UNIT], later[:, UNIT : 2 * UNIT])
        f2 = fetch_factor(2, later[:, 2 * UNIT : 3 * UNIT], later[:, 3 * UNIT :])
        multiply(0, f0)
        multiply(1, f1)
        store(0, False)
        f3 = fetch_factor(3, f0, f1)
        multiply(2, f2)
        store(1, False)
        hand_on(0, nc.sync)
        multiply(3, f3)
        store(2, True)
        hand_on(1, nc.sync)
        hand_on(2, nc.scalar)
        for q in range(4):
            queue = nc.scalar if q % 2 else nc.sync
            queue.dma_start(out=out_2[0, 4 * q : 4 * q + 4, :].bitcast(I32), in_=oqs[32 * q : 32 * q + 4, :].bitcast(I32))
